import numpy as np
import ml_dtypes


def mxq(x, axis, fmt="e4m3"):
    dtype, down = {"e4m3": (ml_dtypes.float8_e4m3fn, 7), "e5m2": (ml_dtypes.float8_e5m2, 14)}[fmt]
    v = np.moveaxis(np.asarray(x, np.float32).astype(ml_dtypes.bfloat16).astype(np.float64), axis, -1)
    blocks = v.reshape(v.shape[:-1] + (-1, 32))
    amax = np.abs(blocks).max(-1, keepdims=True)
    byte = np.maximum(np.where(amax > 0, np.frexp(amax)[1] - 1 + 127, 0) - down, 1)
    scale = np.exp2(byte - 127.0)
    codes = (blocks / scale).astype(np.float32).astype(dtype).astype(np.float64)
    return np.moveaxis((codes * scale).reshape(v.shape), -1, axis)


WIDE = False


def mx_kscale(k):
    if not WIDE:
        return np.ones(k)
    levels = np.array([10, -10, 5, -5, 0])
    if k % 512:
        return np.exp2(np.random.permutation(np.resize(levels, k // 32))).repeat(32)
    a = np.empty((k // 512, 16))
    for p in range(k // 512):
        a[p, :8] = np.random.permutation(np.resize(levels, 8))
        for g in range(8):
            far = levels[np.abs(levels - a[p, g]) >= 10]
            a[p, g + 8] = far[np.random.randint(len(far))]
    return np.exp2(a.ravel()).repeat(32)


BF16 = ml_dtypes.bfloat16


def bf(x):
    return np.asarray(x, np.float32).astype(BF16)


def f64(x):
    return np.asarray(x).astype(np.float64)

def planes(Y):
    n, m = Y.shape
    b = f64(bf(Y)).reshape(n // 32, 32, m)
    amax = np.abs(b).max(1)
    byte = np.clip(np.where(amax > 0, np.frexp(amax)[1] - 1 + 127 - 7, 1), 1, 254)
    codes = (b * np.exp2(127.0 - byte)[:, None, :]).reshape(n, m).astype(np.float32).astype(ml_dtypes.float8_e4m3fn).view(np.uint8)
    words = codes.reshape(n // 512, 128, 4, m).transpose(0, 1, 3, 2)
    return np.ascontiguousarray(words), np.ascontiguousarray(byte.astype(np.uint8).reshape(n // 512, 16, m))


N, P, Q, C = 1024, 1024, 1024, 2

BANDWIDTH = 0.5


def bartlett_kernel(c):
    dist = np.abs(c[:, None] - c[None, :])
    return np.maximum(0.0, 1.0 - dist / BANDWIDTH)


def setup_inputs():
    s, t = mx_kscale(N), mx_kscale(N)
    return {
        "x1": bf(np.random.standard_normal((N, P)) / t[:, None]),
        "x2": bf(np.random.standard_normal((N, Q)) / s[:, None]),
        "e1": bf(np.random.standard_normal(N) * t),
        "e2": bf(np.random.standard_normal(N) * s),
        "coord": bf(np.random.uniform(0.0, 1.0, (N, C))),
    }


def core(x1, x2, e1, e2, coord):
    x1, x2, e1, e2, coord = f64(x1), f64(x2), f64(e1), f64(e2), f64(coord)
    root_n = np.sqrt(x1.shape[0])

    k0 = bartlett_kernel(coord[:, 0])
    k1 = bartlett_kernel(coord[:, 1])
    k = k0 * k1

    ke = k * e2[None, :]

    m = (mxq(ke, 1, "e4m3") @ mxq(x2, 0, "e4m3")) / root_n

    me = e1[:, None] * m

    return (mxq(x1, 0, "e4m3").T @ mxq(me, 0, "e4m3")) / root_n


def reference(x1, x2, e1, e2, coord):
    R_out = core(x1, x2, e1, e2, coord)
    words, scales = planes(R_out)
    return R_out, words, scales

@@ -1,0 +1,272 @@
+from contextlib import ExitStack
+
+import concourse.mybir as mybir
+from concourse.masks import make_identity
+
+N = 1024
+P = 128
+PACK = 4
+HALF = 512
+FLOPS = 2 * 2 * N * N * N
+
+F32 = mybir.dt.float32
+BF16 = mybir.dt.bfloat16
+U32 = mybir.dt.uint32
+I32 = mybir.dt.int32
+U8 = mybir.dt.uint8
+FP8X4 = mybir.dt.float8_e4m3fn_x4
+ALU = mybir.AluOpType
+ACT = mybir.ActivationFunctionType
+INV_ROOT = 1.0 / 32.0
+
+
+def tile_conleyspatialhaccrossequationmeat_x1_kernel(tc, x1, x2, e1, e2, coord, out_0, out_1, out_2):
+    nc = tc.nc
+    with ExitStack() as ctx:
+        const = ctx.enter_context(tc.tile_pool(name="const", bufs=1))
+        keep = ctx.enter_context(tc.tile_pool(name="keep", bufs=1))
+        work = ctx.enter_context(tc.tile_pool(name="work", bufs=3))
+        psum = ctx.enter_context(tc.psum_pool(name="psum", bufs=1))
+
+        ctx.enter_context(tc.manual_schedule())
+        ccol = const.tile([P, 2, 2 * PACK], BF16, name="ccol")
+        nc.sync.dma_start(out=ccol[:], in_=coord.rearrange("(g p t) c -> p g (t c)", g=2, t=PACK))
+        e2col = const.tile([P, 2, PACK], BF16, name="e2col")
+        nc.scalar.dma_start(out=e2col[:], in_=e2.rearrange("(g p t) -> p g t", g=2, t=PACK))
+        e1col = const.tile([P, 2, PACK], BF16, name="e1col")
+        nc.scalar.dma_start(out=e1col[:], in_=e1.rearrange("(g p t) -> p g t", g=2, t=PACK))
+        x2raw = keep.tile([P, 2, PACK, N], BF16, name="x2raw")
+        x1raw = keep.tile([P, 2, PACK, N], BF16, name="x1raw")
+        for src, dst in ((x2, x2raw), (x1, x1raw)):
+            view = src.rearrange("(g p t) w -> g p t w", g=2, t=PACK)
+            for g in range(2):
+                for t2 in range(2):
+                    nc.sync.dma_start(out=dst[:, g, 2 * t2 : 2 * t2 + 2, :], in_=view[g, :, 2 * t2 : 2 * t2 + 2, :])
+
+        ident = const.tile([P, P], BF16, name="ident")
+        make_identity(nc, ident[:])
+        ident_f = const.tile([P, P], F32, name="ident_f")
+        make_identity(nc, ident_f[:])
+        ones = const.tile([P, P], BF16, name="ones")
+        nc.vector.memset(ones[:], 1.0)
+        nb = const.tile([P, 2, 2 * PACK], F32, name="nb")
+        nc.vector.tensor_scalar(out=nb[:], in0=ccol[:], scalar1=-2.0, scalar2=None, op0=ALU.mult)
+        rows = {}
+        for h in range(2):
+            for c in (1, 0):
+                diag = work.tile([P, PACK, P], BF16, name="diag")
+                for u in range(PACK):
+                    k = 2 * u + c
+                    nc.vector.tensor_scalar(out=diag[:, u, :], in0=ident[:], scalar1=ccol[:, h, k : k + 1], scalar2=None, op0=ALU.mult)
+                rows[h, c] = psum.tile([P, HALF], F32, name="row%d%d" % (h, c), tag="b%d" % (2 * h + c))
+                nc.tensor.matmul(rows[h, c][:], ones[:], diag[:].rearrange("p u m -> p (u m)"), start=True, stop=True)
+        ae2 = const.tile([P, 2, PACK], F32, name="ae2")
+        nc.vector.scalar_tensor_tensor(out=ae2[:], in0=e2col[:], scalar=-1.0, in1=e2col[:], op0=ALU.mult, op1=ALU.max)
+        nae2 = const.tile([P, 2, PACK], F32, name="nae2")
+        nc.vector.tensor_scalar(out=nae2[:], in0=ae2[:], scalar1=-1.0, scalar2=None, op0=ALU.mult)
+        sg = const.tile([P, 2, PACK], F32, name="sg")
+        nc.vector.tensor_scalar(out=sg[:], in0=e2col[:], scalar1=0.0, scalar2=-2.0, op0=ALU.is_ge, op1=ALU.mult)
+        nsg = const.tile([P, 2, PACK], F32, name="nsg")
+        nc.vector.tensor_scalar(out=nsg[:], in0=sg[:], scalar1=1.0, scalar2=None, op0=ALU.add)
+        e1s = const.tile([P, 2, PACK], F32, name="e1s")
+        nc.vector.tensor_scalar(out=e1s[:], in0=e1col[:], scalar1=INV_ROOT, scalar2=None, op0=ALU.mult)
+
+        bank_no = [0]
+
+        def new_bank(shape, first, last):
+            k = first + bank_no[0] % (last - first)
+            bank_no[0] += 1
+            return psum.tile(shape, F32, name="bank", tag="b%d" % k)
+
+        ke_c, ke_s, x2_c, x2_s, x1_c, x1_s, me_c, me_s = {}, {}, {}, {}, {}, {}, {}, {}
+
+        def quant(codes, scales, key, src, nm):
+            codes[key] = keep.tile([P, HALF], U32, name="%s_c%d%d" % ((nm,) + key), align_bytes=64)
+            scales[key] = keep.tile([P, HALF], U8, name="%s_s%d%d" % ((nm,) + key), align_bytes=64)
+            nc.vector.quantize_mx(out=codes[key][:].bitcast(FP8X4), scales=scales[key][:], in_=src[:])
+
+        def sign_x2(g):
+            for t in range(PACK):
+                nc.vector.tensor_scalar(out=x2raw[:, g, t, :], in0=x2raw[:, g, t, :], scalar1=nsg[:, g, t : t + 1], scalar2=None, op0=ALU.mult)
+
+        def inter_x2(g, qh):
+            xi = work.tile([P, HALF * PACK], BF16, name="x2i", align_bytes=64)
+            nc.vector.tensor_copy(
+                out=xi[:].rearrange("p (c i t) -> p c t i", t=PACK, i=4),
+                in_=x2raw[:, g, :, qh * HALF : (qh + 1) * HALF].rearrange("p t (c i) -> p c t i", i=4),
+            )
+            return xi
+
+        def inter_x1(h, gg, eng):
+            xi = work.tile([P, HALF * PACK], BF16, name="x1i", align_bytes=64)
+            for u in range(PACK):
+                dst = xi[:, u * HALF : (u + 1) * HALF].rearrange("p (m t) -> p m t", t=PACK)
+                src = x1raw[:, h, :, gg * HALF + u : (gg + 1) * HALF : PACK].rearrange("p t m -> p m t")
+                if eng == "s":
+                    nc.scalar.copy(out=dst, in_=src)
+                else:
+                    nc.vector.tensor_copy(out=dst, in_=src)
+            return xi
+
+        def tri(h, g):
+            a0 = work.tile([P, PACK, HALF], F32, name="a0")
+            r1 = work.tile([P, PACK, HALF], F32, name="r1")
+            a1 = work.tile([P, PACK, HALF], F32, name="a1", bufs=2)
+
+            for t in range(PACK):
+                nc.scalar.activation(out=a1[:, t, :], in_=rows[h, 1][:], func=ACT.Abs, scale=2.0, bias=nb[:, g, 2 * t + 1 : 2 * t + 2])
+                nc.scalar.activation(out=a0[:, t, :], in_=rows[h, 0][:], func=ACT.Abs, scale=2.0, bias=nb[:, g, 2 * t : 2 * t + 1])
+                nc.scalar.activation(out=r1[:, t, :], in_=a1[:, t, :], func=ACT.Relu, scale=nae2[:, g, t : t + 1], bias=ae2[:, g, t : t + 1])
+            return a0, a1, r1
+
+        def clamp(a0):
+            nc.vector.tensor_scalar(out=a0[:], in0=a0[:], scalar1=1.0, scalar2=1.0, op0=ALU.min, op1=ALU.subtract)
+
+        def mirror_second(a1):
+            r1 = work.tile([P, PACK, HALF], F32, name="r1")
+            for t in range(PACK):
+                bank = new_bank([P, PACK, P], 4, 8)
+                for u in range(PACK):
+                    nc.tensor.transpose(bank[:, u, :], a1[:, u, t * P : (t + 1) * P], ident_f[:])
+                nc.scalar.activation(out=r1[:, t, :], in_=bank[:].rearrange("p u m -> p (u m)"), func=ACT.Relu, scale=nae2[:, 1, t : t + 1], bias=ae2[:, 1, t : t + 1])
+            return r1
+
+        def mirror_product(ki, a0, r1, u):
+            bank = new_bank([P, PACK, P], 4, 8)
+            for t in range(PACK):
+                nc.tensor.transpose(bank[:, t, :], a0[:, u, t * P : (t + 1) * P], ident_f[:])
+            nc.vector.tensor_tensor(
+                out=ki[:, u * HALF : (u + 1) * HALF].rearrange("p (c i t) -> p c t i", t=PACK, i=4),
+                in0=bank[:].rearrange("p t (c i) -> p c t i", i=4),
+                in1=r1[:, :, u * P : (u + 1) * P].rearrange("p t (c i) -> p c t i", i=4),
+                op=ALU.mult,
+            )
+
+        def product(a0, r1):
+            ki = work.tile([P, HALF * PACK], BF16, name="kei", align_bytes=64)
+            nc.vector.tensor_tensor(
+                out=ki[:].rearrange("p (c i t) -> p c t i", t=PACK, i=4),
+                in0=a0[:].rearrange("p t (c i) -> p c t i", i=4),
+                in1=r1[:].rearrange("p t (c i) -> p c t i", i=4),
+                op=ALU.mult,
+            )
+            return ki
+
+        def stage1(h, qh, s):
+            bank = new_bank([P, PACK, P], 4 if h == 0 else 0, 8)
+            for u in range(PACK):
+                for g in range(2):
+                    nc.tensor.matmul_mx(
+                        out=bank[:, u, :],
+                        lhsT=ke_c[h, g][:, u * P : (u + 1) * P].bitcast(FP8X4),
+                        lhsT_scale=ke_s[h, g][:, u * P : (u + 1) * P],
+                        rhs=x2_c[g, qh][:, s * P : (s + 1) * P].bitcast(FP8X4),
+                        rhs_scale=x2_s[g, qh][:, s * P : (s + 1) * P],
+                        start=(g == 0),
+                        stop=(g == 1),
+                    )
+            return bank
+
+        def me_out(mi, bank, h, s):
+            nc.vector.tensor_tensor(
+                out=mi[:, s * HALF : (s + 1) * HALF].rearrange("p (n t) -> p n t", t=PACK),
+                in0=bank[:].rearrange("p t n -> p n t"),
+                in1=e1s[:, h : h + 1, :].to_broadcast([P, P, PACK]),
+                op=ALU.mult,
+            )
+
+        a00 = tri(0, 0)
+        sign_x2(0)
+        p00 = inter_x2(0, 0)
+        p01 = inter_x2(0, 1)
+        quant(x2_c, x2_s, (0, 0), p00, "x2")
+        a10 = tri(1, 0)
+        sign_x2(1)
+        clamp(a00[0])
+        quant(x2_c, x2_s, (0, 1), p01, "x2")
+        p10 = inter_x2(1, 0)
+        k00 = product(a00[0], a00[2])
+        quant(x2_c, x2_s, (1, 0), p10, "x2")
+        p11 = inter_x2(1, 1)
+        quant(ke_c, ke_s, (0, 0), k00, "ke")
+        quant(x2_c, x2_s, (1, 1), p11, "x2")
+        w00 = inter_x1(0, 0, "v")
+        r01 = mirror_second(a10[1])
+        a11 = tri(1, 1)
+        clamp(a10[0])
+        quant(x1_c, x1_s, (0, 0), w00, "x1")
+        k01 = work.tile([P, HALF * PACK], BF16, name="kei", align_bytes=64)
+        for u in range(PACK):
+            mirror_product(k01, a10[0], r01, u)
+        k10 = product(a10[0], a10[2])
+        quant(ke_c, ke_s, (0, 1), k01, "ke")
+        quant(ke_c, ke_s, (1, 0), k10, "ke")
+        w01 = inter_x1(0, 1, "s")
+        w10 = inter_x1(1, 0, "s")
+
+        def me_half(h, qh, between):
+            mi = work.tile([P, HALF * PACK], BF16, name="mei", align_bytes=64)
+            for s in range(PACK):
+                me_out(mi, stage1(h, qh, s), h, s)
+                if s in between:
+                    between[s]()
+            return mi
+
+        m00 = me_half(0, 0, {})
+        clamp(a11[0])
+        quant(me_c, me_s, (0, 0), m00, "me")
+        k11 = product(a11[0], a11[2])
+        w11 = inter_x1(1, 1, "s")
+        m01 = me_half(0, 1, {0: lambda: quant(ke_c, ke_s, (1, 1), k11, "ke"), 2: lambda: quant(x1_c, x1_s, (0, 1), w01, "x1")})
+        m10 = me_half(1, 0, {0: lambda: quant(me_c, me_s, (0, 1), m01, "me"), 2: lambda: quant(x1_c, x1_s, (1, 0), w10, "x1")})
+        m11 = me_half(1, 1, {0: lambda: quant(me_c, me_s, (1, 0), m10, "me"), 1: lambda: quant(x1_c, x1_s, (1, 1), w11, "x1")})
+
+        def stage2(qh, gg, u):
+            bank = new_bank([P, HALF], 0, 8)
+            for h in range(2):
+                nc.tensor.matmul_mx(
+                    out=bank[:],
+                    lhsT=x1_c[h, gg][:, u * P : (u + 1) * P].bitcast(FP8X4),
+                    lhsT_scale=x1_s[h, gg][:, u * P : (u + 1) * P],
+                    rhs=me_c[h, qh][:].bitcast(FP8X4),
+                    rhs_scale=me_s[h, qh][:],
+                    start=(h == 0),
+                    stop=(h == 1),
+                )
+            return bank
+
+        osc = [keep.tile([P, 2, HALF], U8, name="osc%d" % qh, align_bytes=64) for qh in range(2)]
+
+        def finish(qh, gg, oi):
+            q0 = qh * HALF
+            oc = work.tile([P, HALF], U32, name="oc", align_bytes=64)
+            nc.vector.quantize_mx(out=oc[:].bitcast(FP8X4), scales=osc[qh][:, gg, :], in_=oi[:])
+            nc.sync.dma_start(
+                out=out_1[gg, :, q0 : q0 + HALF, :].rearrange("p m t -> p (m t)").bitcast(I32), in_=oc[:].bitcast(I32)
+            )
+            if gg == 1:
+                for quad in range(4):
+                    nc.sync.dma_start(
+                        out=out_2[:, 4 * quad : 4 * quad + 4, q0 : q0 + HALF].rearrange("g r m -> r g m").bitcast(I32),
+                        in_=osc[qh][32 * quad : 32 * quad + 4, :, :].bitcast(I32),
+                    )
+
+        early = [stage2(0, 0, 0), stage2(0, 0, 1)]
+        quant(me_c, me_s, (1, 1), m11, "me")
+        last = None
+        for qh in range(2):
+            for gg in range(2):
+                q0 = qh * HALF
+                of = work.tile([P, PACK, HALF], F32, name="of")
+                for u in range(PACK):
+                    bank = early.pop(0) if early else stage2(qh, gg, u)
+                    nc.scalar.activation(out=of[:, u, :], in_=bank[:], func=ACT.Copy, scale=INV_ROOT)
+                nc.sync.dma_start(
+                    out=out_0[gg * HALF : (gg + 1) * HALF, q0 : q0 + HALF].rearrange("(p t) q -> p t q", t=PACK), in_=of[:]
+                )
+                if last is not None:
+                    finish(*last)
+                oi = work.tile([P, HALF * PACK], BF16, name="oi", align_bytes=64)
+                nc.vector.tensor_copy(out=oi[:].rearrange("p (c i t) -> p c t i", t=PACK, i=4), in_=of[:].rearrange("p t (c i) -> p c t i", i=4))
+                last = (qh, gg, oi)
+        finish(*last)

@@ -27,8 +27,8 @@ def tile_conleyspatialhaccrossequationmeat_x1_kernel(tc, x1, x2, e1, e2, coord, 
         keep = ctx.enter_context(tc.tile_pool(name="keep", bufs=1))
         work = ctx.enter_context(tc.tile_pool(name="work", bufs=3))
         psum = ctx.enter_context(tc.psum_pool(name="psum", bufs=1))
-
         ctx.enter_context(tc.manual_schedule())
+
         ccol = const.tile([P, 2, 2 * PACK], BF16, name="ccol")
         nc.sync.dma_start(out=ccol[:], in_=coord.rearrange("(g p t) c -> p g (t c)", g=2, t=PACK))
         e2col = const.tile([P, 2, PACK], BF16, name="e2col")
@@ -49,224 +49,308 @@ def tile_conleyspatialhaccrossequationmeat_x1_kernel(tc, x1, x2, e1, e2, coord, 
         make_identity(nc, ident_f[:])
         ones = const.tile([P, P], BF16, name="ones")
         nc.vector.memset(ones[:], 1.0)
-        nb = const.tile([P, 2, 2 * PACK], F32, name="nb")
-        nc.vector.tensor_scalar(out=nb[:], in0=ccol[:], scalar1=-2.0, scalar2=None, op0=ALU.mult)
-        rows = {}
-        for h in range(2):
-            for c in (1, 0):
-                diag = work.tile([P, PACK, P], BF16, name="diag")
-                for u in range(PACK):
-                    k = 2 * u + c
-                    nc.vector.tensor_scalar(out=diag[:, u, :], in0=ident[:], scalar1=ccol[:, h, k : k + 1], scalar2=None, op0=ALU.mult)
-                rows[h, c] = psum.tile([P, HALF], F32, name="row%d%d" % (h, c), tag="b%d" % (2 * h + c))
-                nc.tensor.matmul(rows[h, c][:], ones[:], diag[:].rearrange("p u m -> p (u m)"), start=True, stop=True)
-        ae2 = const.tile([P, 2, PACK], F32, name="ae2")
-        nc.vector.scalar_tensor_tensor(out=ae2[:], in0=e2col[:], scalar=-1.0, in1=e2col[:], op0=ALU.mult, op1=ALU.max)
-        nae2 = const.tile([P, 2, PACK], F32, name="nae2")
-        nc.vector.tensor_scalar(out=nae2[:], in0=ae2[:], scalar1=-1.0, scalar2=None, op0=ALU.mult)
-        sg = const.tile([P, 2, PACK], F32, name="sg")
-        nc.vector.tensor_scalar(out=sg[:], in0=e2col[:], scalar1=0.0, scalar2=-2.0, op0=ALU.is_ge, op1=ALU.mult)
-        nsg = const.tile([P, 2, PACK], F32, name="nsg")
-        nc.vector.tensor_scalar(out=nsg[:], in0=sg[:], scalar1=1.0, scalar2=None, op0=ALU.add)
-        e1s = const.tile([P, 2, PACK], F32, name="e1s")
-        nc.vector.tensor_scalar(out=e1s[:], in0=e1col[:], scalar1=INV_ROOT, scalar2=None, op0=ALU.mult)
 
-        bank_no = [0]
-
-        def new_bank(shape, first, last):
-            k = first + bank_no[0] % (last - first)
-            bank_no[0] += 1
+        def bank(k, shape):
             return psum.tile(shape, F32, name="bank", tag="b%d" % k)
 
-        ke_c, ke_s, x2_c, x2_s, x1_c, x1_s, me_c, me_s = {}, {}, {}, {}, {}, {}, {}, {}
+        rows = {}
 
-        def quant(codes, scales, key, src, nm):
-            codes[key] = keep.tile([P, HALF], U32, name="%s_c%d%d" % ((nm,) + key), align_bytes=64)
-            scales[key] = keep.tile([P, HALF], U8, name="%s_s%d%d" % ((nm,) + key), align_bytes=64)
+        def make_row(h, c):
+            diag = work.tile([P, PACK, P], BF16, name="diag")
+            for u in range(PACK):
+                k = 2 * u + c
+                nc.vector.tensor_scalar(out=diag[:, u, :], in0=ident[:], scalar1=ccol[:, h, k : k + 1], scalar2=None, op0=ALU.mult)
+            rows[h, c] = bank(2 * h + c, [P, HALF])
+            nc.tensor.matmul(rows[h, c][:], ones[:], diag[:].rearrange("p u m -> p (u m)"), start=True, stop=True)
+
+        make_row(0, 0)
+        nb = const.tile([P, 2, 2 * PACK], F32, name="nb")
+        nc.vector.tensor_scalar(out=nb[:], in0=ccol[:], scalar1=-2.0, scalar2=None, op0=ALU.mult)
+        make_row(0, 1)
+        ae2 = const.tile([P, 2, PACK], F32, name="ae2")
+        nc.vector.scalar_tensor_tensor(out=ae2[:], in0=e2col[:], scalar=-1.0, in1=e2col[:], op0=ALU.mult, op1=ALU.max)
+        sg = const.tile([P, 2, PACK], F32, name="sg")
+        nc.vector.tensor_scalar(out=sg[:], in0=e2col[:], scalar1=0.0, scalar2=-2.0, op0=ALU.is_ge, op1=ALU.mult)
+        e1s = const.tile([P, 2, PACK], F32, name="e1s")
+        nc.vector.tensor_scalar(out=e1s[:], in0=e1col[:], scalar1=INV_ROOT, scalar2=None, op0=ALU.mult)
+        nae2 = const.tile([P, 2, PACK], F32, name="nae2")
+        nc.vector.tensor_scalar(out=nae2[:], in0=ae2[:], scalar1=-1.0, scalar2=None, op0=ALU.mult)
+        nsg = const.tile([P, 2, PACK], F32, name="nsg")
+        nc.vector.tensor_scalar(out=nsg[:], in0=sg[:], scalar1=1.0, scalar2=None, op0=ALU.add)
+        make_row(1, 0)
+        make_row(1, 1)
+        sdiag = const.tile([P, 2, PACK, P], BF16, name="sdiag")
+        for g in range(2):
+            for t in range(PACK):
+                nc.gpsimd.tensor_scalar(out=sdiag[:, g, t, :], in0=ident[:], scalar1=nsg[:, g, t : t + 1], scalar2=1.0, op0=ALU.mult, op1=ALU.mult)
+
+        codes, scales = {}, {}
+
+        def quant(key, src):
+            codes[key] = keep.tile([P, HALF], U32, name="c_%s%d%d" % key, align_bytes=64)
+            scales[key] = keep.tile([P, HALF], U8, name="s_%s%d%d" % key, align_bytes=64)
             nc.vector.quantize_mx(out=codes[key][:].bitcast(FP8X4), scales=scales[key][:], in_=src[:])
+
+        def mx(out, lkey, lcol, rkey, rcol, rn, first, last):
+            nc.tensor.matmul_mx(
+                out=out,
+                lhsT=codes[lkey][:, lcol : lcol + P].bitcast(FP8X4),
+                lhsT_scale=scales[lkey][:, lcol : lcol + P],
+                rhs=codes[rkey][:, rcol : rcol + rn].bitcast(FP8X4),
+                rhs_scale=scales[rkey][:, rcol : rcol + rn],
+                start=first,
+                stop=last,
+            )
+
+        def lanes(ap):
+            return ap.rearrange("p (c i t) -> p c t i", t=PACK, i=4)
+
+        def runs(ap):
+            return ap.rearrange("p t (c i) -> p c t i", i=4)
+
+        def packed(name):
+            return work.tile([P, HALF * PACK], BF16, name=name, align_bytes=64)
 
         def sign_x2(g):
             for t in range(PACK):
-                nc.vector.tensor_scalar(out=x2raw[:, g, t, :], in0=x2raw[:, g, t, :], scalar1=nsg[:, g, t : t + 1], scalar2=None, op0=ALU.mult)
+                nc.vector.tensor_scalar(out=x2raw[:, g, t, 0:HALF], in0=x2raw[:, g, t, 0:HALF], scalar1=nsg[:, g, t : t + 1], scalar2=None, op0=ALU.mult)
 
-        def inter_x2(g, qh):
-            xi = work.tile([P, HALF * PACK], BF16, name="x2i", align_bytes=64)
+        def inter_x2(g):
+            xi = packed("x2i")
+            nc.vector.tensor_copy(out=lanes(xi[:]), in_=runs(x2raw[:, g, :, 0:HALF]))
+            return xi
+
+        def x2_banks(g):
+            res = []
+            for s in range(PACK):
+                b = bank(4 + s, [P, PACK, P])
+                for t in range(PACK):
+                    nc.tensor.matmul(b[:, t, :], sdiag[:, g, t, :], x2raw[:, g, t, HALF + s * P : HALF + (s + 1) * P], start=True, stop=True)
+                res.append(b)
+            return res
+
+        def x2_out(banks):
+            xi = packed("x2i")
+            for s in range(PACK):
+                nc.scalar.copy(out=xi[:, s * HALF : (s + 1) * HALF].rearrange("p (n t) -> p n t", t=PACK), in_=banks[s][:].rearrange("p t n -> p n t"))
+            return xi
+
+        def inter_x1(h, gg):
+            xi = packed("x1i")
             nc.vector.tensor_copy(
-                out=xi[:].rearrange("p (c i t) -> p c t i", t=PACK, i=4),
-                in_=x2raw[:, g, :, qh * HALF : (qh + 1) * HALF].rearrange("p t (c i) -> p c t i", i=4),
+                out=xi[:].rearrange("p (u m t) -> p u m t", u=PACK, t=PACK),
+                in_=x1raw[:, h, :, gg * HALF : (gg + 1) * HALF].rearrange("p t (m u) -> p u m t", u=PACK),
             )
             return xi
 
-        def inter_x1(h, gg, eng):
-            xi = work.tile([P, HALF * PACK], BF16, name="x1i", align_bytes=64)
-            for u in range(PACK):
-                dst = xi[:, u * HALF : (u + 1) * HALF].rearrange("p (m t) -> p m t", t=PACK)
-                src = x1raw[:, h, :, gg * HALF + u : (gg + 1) * HALF : PACK].rearrange("p t m -> p m t")
-                if eng == "s":
-                    nc.scalar.copy(out=dst, in_=src)
-                else:
-                    nc.vector.tensor_copy(out=dst, in_=src)
-            return xi
-
         def tri(h, g):
-            a0 = work.tile([P, PACK, HALF], F32, name="a0")
-            r1 = work.tile([P, PACK, HALF], F32, name="r1")
+            a0 = work.tile([P, PACK, HALF], F32, name="a0", tag="a0")
             a1 = work.tile([P, PACK, HALF], F32, name="a1", bufs=2)
-
+            r1 = work.tile([P, PACK, HALF], F32, name="r1", bufs=4)
+            for t in range(PACK):
+                nc.scalar.activation(out=a0[:, t, :], in_=rows[h, 0][:], func=ACT.Abs, scale=2.0, bias=nb[:, g, 2 * t : 2 * t + 1])
             for t in range(PACK):
                 nc.scalar.activation(out=a1[:, t, :], in_=rows[h, 1][:], func=ACT.Abs, scale=2.0, bias=nb[:, g, 2 * t + 1 : 2 * t + 2])
-                nc.scalar.activation(out=a0[:, t, :], in_=rows[h, 0][:], func=ACT.Abs, scale=2.0, bias=nb[:, g, 2 * t : 2 * t + 1])
+            for t in range(PACK):
                 nc.scalar.activation(out=r1[:, t, :], in_=a1[:, t, :], func=ACT.Relu, scale=nae2[:, g, t : t + 1], bias=ae2[:, g, t : t + 1])
             return a0, a1, r1
 
         def clamp(a0):
             nc.vector.tensor_scalar(out=a0[:], in0=a0[:], scalar1=1.0, scalar2=1.0, op0=ALU.min, op1=ALU.subtract)
 
-        def mirror_second(a1):
-            r1 = work.tile([P, PACK, HALF], F32, name="r1")
-            for t in range(PACK):
-                bank = new_bank([P, PACK, P], 4, 8)
-                for u in range(PACK):
-                    nc.tensor.transpose(bank[:, u, :], a1[:, u, t * P : (t + 1) * P], ident_f[:])
-                nc.scalar.activation(out=r1[:, t, :], in_=bank[:].rearrange("p u m -> p (u m)"), func=ACT.Relu, scale=nae2[:, 1, t : t + 1], bias=ae2[:, 1, t : t + 1])
-            return r1
-
-        def mirror_product(ki, a0, r1, u):
-            bank = new_bank([P, PACK, P], 4, 8)
-            for t in range(PACK):
-                nc.tensor.transpose(bank[:, t, :], a0[:, u, t * P : (t + 1) * P], ident_f[:])
-            nc.vector.tensor_tensor(
-                out=ki[:, u * HALF : (u + 1) * HALF].rearrange("p (c i t) -> p c t i", t=PACK, i=4),
-                in0=bank[:].rearrange("p t (c i) -> p c t i", i=4),
-                in1=r1[:, :, u * P : (u + 1) * P].rearrange("p t (c i) -> p c t i", i=4),
-                op=ALU.mult,
-            )
-
         def product(a0, r1):
-            ki = work.tile([P, HALF * PACK], BF16, name="kei", align_bytes=64)
-            nc.vector.tensor_tensor(
-                out=ki[:].rearrange("p (c i t) -> p c t i", t=PACK, i=4),
-                in0=a0[:].rearrange("p t (c i) -> p c t i", i=4),
-                in1=r1[:].rearrange("p t (c i) -> p c t i", i=4),
-                op=ALU.mult,
-            )
+            ki = packed("kei")
+            nc.vector.tensor_tensor(out=lanes(ki[:]), in0=runs(a0[:]), in1=runs(r1[:]), op=ALU.mult)
             return ki
 
-        def stage1(h, qh, s):
-            bank = new_bank([P, PACK, P], 4 if h == 0 else 0, 8)
-            for u in range(PACK):
-                for g in range(2):
-                    nc.tensor.matmul_mx(
-                        out=bank[:, u, :],
-                        lhsT=ke_c[h, g][:, u * P : (u + 1) * P].bitcast(FP8X4),
-                        lhsT_scale=ke_s[h, g][:, u * P : (u + 1) * P],
-                        rhs=x2_c[g, qh][:, s * P : (s + 1) * P].bitcast(FP8X4),
-                        rhs_scale=x2_s[g, qh][:, s * P : (s + 1) * P],
-                        start=(g == 0),
-                        stop=(g == 1),
-                    )
-            return bank
+        def mirror_second(a1):
+            r1 = work.tile([P, PACK, HALF], F32, name="r1", bufs=4)
+            for t in range(PACK):
+                b = bank(t, [P, PACK, P])
+                for u in range(PACK):
+                    nc.tensor.transpose(b[:, u, :], a1[:, u, t * P : (t + 1) * P], ident_f[:])
+                nc.scalar.activation(out=r1[:, t, :], in_=b[:].rearrange("p u m -> p (u m)"), func=ACT.Relu, scale=nae2[:, 1, t : t + 1], bias=ae2[:, 1, t : t + 1])
+            return r1
 
-        def me_out(mi, bank, h, s):
+        def mirror_banks(a0):
+            res = []
+            for u in range(PACK):
+                b = bank(u, [P, PACK, P])
+                for t in range(PACK):
+                    nc.tensor.transpose(b[:, t, :], a0[:, u, t * P : (t + 1) * P], ident_f[:])
+                res.append(b)
+            return res
+
+        def mirror_product(banks, r1):
+            ki = packed("kei")
+            for u in range(PACK):
+                nc.vector.tensor_tensor(out=lanes(ki[:, u * HALF : (u + 1) * HALF]), in0=runs(banks[u][:]), in1=runs(r1[:, :, u * P : (u + 1) * P]), op=ALU.mult)
+            return ki
+
+        def stage1_narrow(h, qh, first_bank):
+            res = []
+            for s in range(PACK):
+                b = bank(first_bank + s, [P, PACK, P])
+                for u in range(PACK):
+                    for g in range(2):
+                        mx(b[:, u, :], ("k", h, g), u * P, ("x2", g, qh), s * P, P, g == 0, g == 1)
+                res.append(b)
+            return res
+
+        def me_narrow(mi, b, h, s):
             nc.vector.tensor_tensor(
                 out=mi[:, s * HALF : (s + 1) * HALF].rearrange("p (n t) -> p n t", t=PACK),
-                in0=bank[:].rearrange("p t n -> p n t"),
+                in0=b[:].rearrange("p t n -> p n t"),
                 in1=e1s[:, h : h + 1, :].to_broadcast([P, P, PACK]),
                 op=ALU.mult,
             )
 
-        a00 = tri(0, 0)
-        sign_x2(0)
-        p00 = inter_x2(0, 0)
-        p01 = inter_x2(0, 1)
-        quant(x2_c, x2_s, (0, 0), p00, "x2")
-        a10 = tri(1, 0)
-        sign_x2(1)
-        clamp(a00[0])
-        quant(x2_c, x2_s, (0, 1), p01, "x2")
-        p10 = inter_x2(1, 0)
-        k00 = product(a00[0], a00[2])
-        quant(x2_c, x2_s, (1, 0), p10, "x2")
-        p11 = inter_x2(1, 1)
-        quant(ke_c, ke_s, (0, 0), k00, "ke")
-        quant(x2_c, x2_s, (1, 1), p11, "x2")
-        w00 = inter_x1(0, 0, "v")
-        r01 = mirror_second(a10[1])
-        a11 = tri(1, 1)
-        clamp(a10[0])
-        quant(x1_c, x1_s, (0, 0), w00, "x1")
-        k01 = work.tile([P, HALF * PACK], BF16, name="kei", align_bytes=64)
-        for u in range(PACK):
-            mirror_product(k01, a10[0], r01, u)
-        k10 = product(a10[0], a10[2])
-        quant(ke_c, ke_s, (0, 1), k01, "ke")
-        quant(ke_c, ke_s, (1, 0), k10, "ke")
-        w01 = inter_x1(0, 1, "s")
-        w10 = inter_x1(1, 0, "s")
+        def me_wide(h, qh, first_bank):
+            mp = work.tile([P, PACK, HALF], BF16, name="mp", bufs=2)
+            for u in range(PACK):
+                b = bank(first_bank + u, [P, HALF])
+                for g in range(2):
+                    mx(b[:], ("k", h, g), u * P, ("x2", g, qh), 0, HALF, g == 0, g == 1)
+                nc.scalar.activation(out=mp[:, u, :], in_=b[:], func=ACT.Copy, scale=e1s[:, h, u : u + 1])
+            return mp
 
-        def me_half(h, qh, between):
-            mi = work.tile([P, HALF * PACK], BF16, name="mei", align_bytes=64)
-            for s in range(PACK):
-                me_out(mi, stage1(h, qh, s), h, s)
-                if s in between:
-                    between[s]()
+        def inter_me(mp):
+            mi = packed("mei")
+            nc.vector.tensor_copy(out=lanes(mi[:]), in_=runs(mp[:]))
             return mi
 
-        m00 = me_half(0, 0, {})
-        clamp(a11[0])
-        quant(me_c, me_s, (0, 0), m00, "me")
-        k11 = product(a11[0], a11[2])
-        w11 = inter_x1(1, 1, "s")
-        m01 = me_half(0, 1, {0: lambda: quant(ke_c, ke_s, (1, 1), k11, "ke"), 2: lambda: quant(x1_c, x1_s, (0, 1), w01, "x1")})
-        m10 = me_half(1, 0, {0: lambda: quant(me_c, me_s, (0, 1), m01, "me"), 2: lambda: quant(x1_c, x1_s, (1, 0), w10, "x1")})
-        m11 = me_half(1, 1, {0: lambda: quant(me_c, me_s, (1, 0), m10, "me"), 1: lambda: quant(x1_c, x1_s, (1, 1), w11, "x1")})
+        t00 = tri(0, 0)
+        sign_x2(0)
+        p00 = inter_x2(0)
+        clamp(t00[0])
+        sign_x2(1)
+        quant(("x2", 0, 0), p00)
+        p10 = inter_x2(1)
+        xb0 = x2_banks(0)
+        t10 = tri(1, 0)
+        w00 = inter_x1(0, 0)
+        quant(("x2", 1, 0), p10)
+        k00 = product(t00[0], t00[2])
+        w01 = inter_x1(0, 1)
+        clamp(t10[0])
+        quant(("k", 0, 0), k00)
+        t11 = tri(1, 1)
+        w10 = inter_x1(1, 0)
+        k10 = product(t10[0], t10[2])
+        quant(("x1", 0, 0), w00)
+        w11 = inter_x1(1, 1)
+        clamp(t11[0])
+        quant(("k", 1, 0), k10)
+        r01 = mirror_second(t10[1])
+        mb = mirror_banks(t10[0])
+        quant(("x1", 0, 1), w01)
+        k11 = product(t11[0], t11[2])
+        quant(("x1", 1, 0), w10)
+        quant(("k", 1, 1), k11)
+        k01 = mirror_product(mb, r01)
+        p01 = x2_out(xb0)
+        p11 = x2_out(x2_banks(1))
+        quant(("x1", 1, 1), w11)
+        quant(("k", 0, 1), k01)
+        m10 = packed("mei")
+        nb10 = stage1_narrow(1, 0, 0)
+        for s in range(PACK):
+            me_narrow(m10, nb10[s], 1, s)
+        quant(("x2", 0, 1), p01)
+        quant(("x2", 1, 1), p11)
+        mp00 = me_wide(0, 0, 4)
+        quant(("me", 1, 0), m10)
+        m00 = inter_me(mp00)
+        mp01 = me_wide(0, 1, 0)
+        nb11 = stage1_narrow(1, 1, 4)
+        m11 = packed("mei")
+        me_narrow(m11, nb11[0], 1, 0)
+        quant(("me", 0, 0), m00)
+        for s in range(1, PACK):
+            me_narrow(m11, nb11[s], 1, s)
+        m01 = inter_me(mp01)
+        quant(("me", 1, 1), m11)
 
-        def stage2(qh, gg, u):
-            bank = new_bank([P, HALF], 0, 8)
-            for h in range(2):
-                nc.tensor.matmul_mx(
-                    out=bank[:],
-                    lhsT=x1_c[h, gg][:, u * P : (u + 1) * P].bitcast(FP8X4),
-                    lhsT_scale=x1_s[h, gg][:, u * P : (u + 1) * P],
-                    rhs=me_c[h, qh][:].bitcast(FP8X4),
-                    rhs_scale=me_s[h, qh][:],
-                    start=(h == 0),
-                    stop=(h == 1),
-                )
-            return bank
+        bank_no = [0]
+
+        def next_bank(shape):
+            bank_no[0] += 1
+            return bank((bank_no[0] - 1) % 8, shape)
 
         osc = [keep.tile([P, 2, HALF], U8, name="osc%d" % qh, align_bytes=64) for qh in range(2)]
 
-        def finish(qh, gg, oi):
+        def product_out(qh, gg, of):
+            for u in range(PACK):
+                b = next_bank([P, HALF])
+                for h in range(2):
+                    mx(b[:], ("x1", h, gg), u * P, ("me", h, qh), 0, HALF, h == 0, h == 1)
+                nc.scalar.activation(out=of[:, u, :], in_=b[:], func=ACT.Copy, scale=INV_ROOT)
+
+        def product_out_split(qh, gg, of, part):
+            w = HALF // 2
+            for u in range(0, PACK, 2):
+                b = next_bank([P, 2, w])
+                for v in range(2):
+                    for h in range(2):
+                        mx(b[:, v, :], ("x1", h, gg), (u + v) * P, ("me", h, qh), part * w, w, h == 0, h == 1)
+                nc.scalar.activation(out=of[:, u : u + 2, part * w : (part + 1) * w], in_=b[:], func=ACT.Copy, scale=INV_ROOT)
+
+        def inter_out(of, c0, c1):
+            oi = work.tile([P, HALF * PACK], BF16, name="oi", tag="kei", align_bytes=64)
+            nc.vector.tensor_copy(out=lanes(oi[:, PACK * c0 : PACK * c1]), in_=runs(of[:, :, c0:c1]))
+            return oi
+
+        def store_f32(qh, gg, of, c0, c1):
+            q0 = qh * HALF
+            nc.sync.dma_start(
+                out=out_0[gg * HALF : (gg + 1) * HALF, q0 + c0 : q0 + c1].rearrange("(p t) q -> p t q", t=PACK), in_=of[:, :, c0:c1]
+            )
+
+        def finish(qh, gg, oi, c0, c1):
             q0 = qh * HALF
             oc = work.tile([P, HALF], U32, name="oc", align_bytes=64)
-            nc.vector.quantize_mx(out=oc[:].bitcast(FP8X4), scales=osc[qh][:, gg, :], in_=oi[:])
+            nc.vector.quantize_mx(out=oc[:, c0:c1].bitcast(FP8X4), scales=osc[qh][:, gg, c0:c1], in_=oi[:, PACK * c0 : PACK * c1])
             nc.sync.dma_start(
-                out=out_1[gg, :, q0 : q0 + HALF, :].rearrange("p m t -> p (m t)").bitcast(I32), in_=oc[:].bitcast(I32)
+                out=out_1[gg, :, q0 + c0 : q0 + c1, :].rearrange("p m t -> p (m t)").bitcast(I32), in_=oc[:, c0:c1].bitcast(I32)
             )
-            if gg == 1:
-                for quad in range(4):
-                    nc.sync.dma_start(
-                        out=out_2[:, 4 * quad : 4 * quad + 4, q0 : q0 + HALF].rearrange("g r m -> r g m").bitcast(I32),
-                        in_=osc[qh][32 * quad : 32 * quad + 4, :, :].bitcast(I32),
-                    )
 
-        early = [stage2(0, 0, 0), stage2(0, 0, 1)]
-        quant(me_c, me_s, (1, 1), m11, "me")
-        last = None
-        for qh in range(2):
-            for gg in range(2):
-                q0 = qh * HALF
-                of = work.tile([P, PACK, HALF], F32, name="of")
-                for u in range(PACK):
-                    bank = early.pop(0) if early else stage2(qh, gg, u)
-                    nc.scalar.activation(out=of[:, u, :], in_=bank[:], func=ACT.Copy, scale=INV_ROOT)
-                nc.sync.dma_start(
-                    out=out_0[gg * HALF : (gg + 1) * HALF, q0 : q0 + HALF].rearrange("(p t) q -> p t q", t=PACK), in_=of[:]
+        def store_scales(qh):
+            q0 = qh * HALF
+            for quad in range(4):
+                eng = nc.sync if quad % 2 == 0 else nc.scalar
+                eng.dma_start(
+                    out=out_2[:, 4 * quad : 4 * quad + 4, q0 : q0 + HALF].rearrange("g r m -> r g m").bitcast(I32),
+                    in_=osc[qh][32 * quad : 32 * quad + 4, :, :].bitcast(I32),
                 )
-                if last is not None:
-                    finish(*last)
-                oi = work.tile([P, HALF * PACK], BF16, name="oi", align_bytes=64)
-                nc.vector.tensor_copy(out=oi[:].rearrange("p (c i t) -> p c t i", t=PACK, i=4), in_=of[:].rearrange("p t (c i) -> p c t i", i=4))
-                last = (qh, gg, oi)
-        finish(*last)
+
+        def out_tile():
+            return work.tile([P, PACK, HALF], F32, name="of", tag="a0")
+
+        of00 = out_tile()
+        product_out(0, 0, of00)
+        store_f32(0, 0, of00, 0, HALF)
+        of01 = out_tile()
+        product_out(0, 1, of01)
+        store_f32(0, 1, of01, 0, HALF)
+        i00 = inter_out(of00, 0, HALF)
+        quant(("me", 0, 1), m01)
+        finish(0, 0, i00, 0, HALF)
+        i01 = inter_out(of01, 0, HALF)
+        of10 = out_tile()
+        product_out(1, 0, of10)
+        store_f32(1, 0, of10, 0, HALF)
+        finish(0, 1, i01, 0, HALF)
+        i10 = inter_out(of10, 0, HALF)
+        of11 = out_tile()
+        product_out_split(1, 1, of11, 0)
+        product_out_split(1, 1, of11, 1)
+        store_scales(0)
+        w = HALF // 2
+        store_f32(1, 1, of11, 0, w)
+        ia = inter_out(of11, 0, w)
+        finish(1, 0, i10, 0, HALF)
+        store_f32(1, 1, of11, w, HALF)
+        ib = inter_out(of11, w, HALF)
+        finish(1, 1, ia, 0, w)
+        finish(1, 1, ib, w, HALF)
+        store_scales(1)

@@ -33,8 +33,6 @@ def tile_conleyspatialhaccrossequationmeat_x1_kernel(tc, x1, x2, e1, e2, coord, 
         nc.sync.dma_start(out=ccol[:], in_=coord.rearrange("(g p t) c -> p g (t c)", g=2, t=PACK))
         e2col = const.tile([P, 2, PACK], BF16, name="e2col")
         nc.scalar.dma_start(out=e2col[:], in_=e2.rearrange("(g p t) -> p g t", g=2, t=PACK))
-        e1col = const.tile([P, 2, PACK], BF16, name="e1col")
-        nc.scalar.dma_start(out=e1col[:], in_=e1.rearrange("(g p t) -> p g t", g=2, t=PACK))
         x2raw = keep.tile([P, 2, PACK, N], BF16, name="x2raw")
         x1raw = keep.tile([P, 2, PACK, N], BF16, name="x1raw")
         for src, dst in ((x2, x2raw), (x1, x1raw)):
@@ -42,6 +40,9 @@ def tile_conleyspatialhaccrossequationmeat_x1_kernel(tc, x1, x2, e1, e2, coord, 
             for g in range(2):
                 for t2 in range(2):
                     nc.sync.dma_start(out=dst[:, g, 2 * t2 : 2 * t2 + 2, :], in_=view[g, :, 2 * t2 : 2 * t2 + 2, :])
+
+        e1col = const.tile([P, 2, PACK], BF16, name="e1col")
+        nc.sync.dma_start(out=e1col[:], in_=e1.rearrange("(g p t) -> p g t", g=2, t=PACK))
 
         ident = const.tile([P, P], BF16, name="ident")
         make_identity(nc, ident[:])
@@ -63,16 +64,14 @@ def tile_conleyspatialhaccrossequationmeat_x1_kernel(tc, x1, x2, e1, e2, coord, 
             rows[h, c] = bank(2 * h + c, [P, HALF])
             nc.tensor.matmul(rows[h, c][:], ones[:], diag[:].rearrange("p u m -> p (u m)"), start=True, stop=True)
 
-        make_row(0, 0)
         nb = const.tile([P, 2, 2 * PACK], F32, name="nb")
         nc.vector.tensor_scalar(out=nb[:], in0=ccol[:], scalar1=-2.0, scalar2=None, op0=ALU.mult)
+        make_row(0, 0)
         make_row(0, 1)
         ae2 = const.tile([P, 2, PACK], F32, name="ae2")
         nc.vector.scalar_tensor_tensor(out=ae2[:], in0=e2col[:], scalar=-1.0, in1=e2col[:], op0=ALU.mult, op1=ALU.max)
         sg = const.tile([P, 2, PACK], F32, name="sg")
         nc.vector.tensor_scalar(out=sg[:], in0=e2col[:], scalar1=0.0, scalar2=-2.0, op0=ALU.is_ge, op1=ALU.mult)
-        e1s = const.tile([P, 2, PACK], F32, name="e1s")
-        nc.vector.tensor_scalar(out=e1s[:], in0=e1col[:], scalar1=INV_ROOT, scalar2=None, op0=ALU.mult)
         nae2 = const.tile([P, 2, PACK], F32, name="nae2")
         nc.vector.tensor_scalar(out=nae2[:], in0=ae2[:], scalar1=-1.0, scalar2=None, op0=ALU.mult)
         nsg = const.tile([P, 2, PACK], F32, name="nsg")
@@ -138,8 +137,8 @@ def tile_conleyspatialhaccrossequationmeat_x1_kernel(tc, x1, x2, e1, e2, coord, 
         def inter_x1(h, gg):
             xi = packed("x1i")
             nc.vector.tensor_copy(
-                out=xi[:].rearrange("p (u m t) -> p u m t", u=PACK, t=PACK),
-                in_=x1raw[:, h, :, gg * HALF : (gg + 1) * HALF].rearrange("p t (m u) -> p u m t", u=PACK),
+                out=xi[:].rearrange("p (u c i t) -> p c u i t", u=PACK, i=2, t=PACK),
+                in_=x1raw[:, h, :, gg * HALF : (gg + 1) * HALF].rearrange("p t (c i u) -> p c u i t", u=PACK, i=2),
             )
             return xi
 
@@ -235,6 +234,8 @@ def tile_conleyspatialhaccrossequationmeat_x1_kernel(tc, x1, x2, e1, e2, coord, 
         clamp(t10[0])
         quant(("k", 0, 0), k00)
         t11 = tri(1, 1)
+        e1s = const.tile([P, 2, PACK], F32, name="e1s")
+        nc.vector.tensor_scalar(out=e1s[:], in0=e1col[:], scalar1=INV_ROOT, scalar2=None, op0=ALU.mult)
         w10 = inter_x1(1, 0)
         k10 = product(t10[0], t10[2])
         quant(("x1", 0, 0), w00)

@@ -7,6 +7,7 @@ N = 1024
 P = 128
 PACK = 4
 HALF = 512
+QUARTER = 256
 FLOPS = 2 * 2 * N * N * N
 
 F32 = mybir.dt.float32
@@ -33,14 +34,18 @@ def tile_conleyspatialhaccrossequationmeat_x1_kernel(tc, x1, x2, e1, e2, coord, 
         nc.sync.dma_start(out=ccol[:], in_=coord.rearrange("(g p t) c -> p g (t c)", g=2, t=PACK))
         e2col = const.tile([P, 2, PACK], BF16, name="e2col")
         nc.scalar.dma_start(out=e2col[:], in_=e2.rearrange("(g p t) -> p g t", g=2, t=PACK))
-        x2raw = keep.tile([P, 2, PACK, N], BF16, name="x2raw")
+        x2lo = [keep.tile([P, PACK, HALF], BF16, name="x2lo%d" % g) for g in range(2)]
+        x2hi = [keep.tile([P, PACK, HALF], BF16, name="x2hi%d" % g) for g in range(2)]
         x1raw = keep.tile([P, 2, PACK, N], BF16, name="x1raw")
-        for src, dst in ((x2, x2raw), (x1, x1raw)):
-            view = src.rearrange("(g p t) w -> g p t w", g=2, t=PACK)
-            for g in range(2):
-                for t2 in range(2):
-                    nc.sync.dma_start(out=dst[:, g, 2 * t2 : 2 * t2 + 2, :], in_=view[g, :, 2 * t2 : 2 * t2 + 2, :])
-
+        x2view = x2.rearrange("(g p t) w -> g p t w", g=2, t=PACK)
+        x1view = x1.rearrange("(g p t) w -> g p t w", g=2, t=PACK)
+        for g in range(2):
+            nc.sync.dma_start(out=x2lo[g][:], in_=x2view[g, :, :, 0:HALF])
+        for g in range(2):
+            for t2 in range(2):
+                nc.sync.dma_start(out=x1raw[:, g, 2 * t2 : 2 * t2 + 2, :], in_=x1view[g, :, 2 * t2 : 2 * t2 + 2, :])
+        for g in range(2):
+            nc.sync.dma_start(out=x2hi[g][:], in_=x2view[g, :, :, HALF:N])
         e1col = const.tile([P, 2, PACK], BF16, name="e1col")
         nc.sync.dma_start(out=e1col[:], in_=e1.rearrange("(g p t) -> p g t", g=2, t=PACK))
 
@@ -57,7 +62,7 @@ def tile_conleyspatialhaccrossequationmeat_x1_kernel(tc, x1, x2, e1, e2, coord, 
         rows = {}
 
         def make_row(h, c):
-            diag = work.tile([P, PACK, P], BF16, name="diag")
+            diag = work.tile([P, PACK, P], BF16, name="diag", bufs=4)
             for u in range(PACK):
                 k = 2 * u + c
                 nc.vector.tensor_scalar(out=diag[:, u, :], in0=ident[:], scalar1=ccol[:, h, k : k + 1], scalar2=None, op0=ALU.mult)
@@ -90,6 +95,18 @@ def tile_conleyspatialhaccrossequationmeat_x1_kernel(tc, x1, x2, e1, e2, coord, 
             scales[key] = keep.tile([P, HALF], U8, name="s_%s%d%d" % key, align_bytes=64)
             nc.vector.quantize_mx(out=codes[key][:].bitcast(FP8X4), scales=scales[key][:], in_=src[:])
 
+        def quant_pair(keys, src):
+            ct = keep.tile([P, 2, HALF], U32, name="c_%s%d%d" % keys[0], align_bytes=64)
+            st = keep.tile([P, 2, HALF], U8, name="s_%s%d%d" % keys[0], align_bytes=64)
+            nc.vector.quantize_mx(
+                out=ct[:].rearrange("p k n -> p (k n)").bitcast(FP8X4),
+                scales=st[:].rearrange("p k n -> p (k n)"),
+                in_=src[:].rearrange("p k n -> p (k n)"),
+            )
+            for k in range(2):
+                codes[keys[k]] = ct[:, k, :]
+                scales[keys[k]] = st[:, k, :]
+
         def mx(out, lkey, lcol, rkey, rcol, rn, first, last):
             nc.tensor.matmul_mx(
                 out=out,
@@ -110,42 +127,39 @@ def tile_conleyspatialhaccrossequationmeat_x1_kernel(tc, x1, x2, e1, e2, coord, 
         def packed(name):
             return work.tile([P, HALF * PACK], BF16, name=name, align_bytes=64)
 
+        def pair(name):
+            return work.tile([P, 2, HALF * PACK], BF16, name=name, tag="pair", bufs=5, align_bytes=64)
+
         def sign_x2(g):
             for t in range(PACK):
-                nc.vector.tensor_scalar(out=x2raw[:, g, t, 0:HALF], in0=x2raw[:, g, t, 0:HALF], scalar1=nsg[:, g, t : t + 1], scalar2=None, op0=ALU.mult)
+                nc.vector.tensor_scalar(out=x2lo[g][:, t, :], in0=x2lo[g][:, t, :], scalar1=nsg[:, g, t : t + 1], scalar2=None, op0=ALU.mult)
 
-        def inter_x2(g):
-            xi = packed("x2i")
-            nc.vector.tensor_copy(out=lanes(xi[:]), in_=runs(x2raw[:, g, :, 0:HALF]))
-            return xi
+        def inter_x2(xi, g):
+            nc.vector.tensor_copy(out=lanes(xi[:, g, :]), in_=runs(x2lo[g][:]))
 
         def x2_banks(g):
             res = []
             for s in range(PACK):
                 b = bank(4 + s, [P, PACK, P])
                 for t in range(PACK):
-                    nc.tensor.matmul(b[:, t, :], sdiag[:, g, t, :], x2raw[:, g, t, HALF + s * P : HALF + (s + 1) * P], start=True, stop=True)
+                    nc.tensor.matmul(b[:, t, :], sdiag[:, g, t, :], x2hi[g][:, t, s * P : (s + 1) * P], start=True, stop=True)
                 res.append(b)
             return res
 
-        def x2_out(banks):
-            xi = packed("x2i")
+        def x2_out(xi, g, banks):
             for s in range(PACK):
-                nc.scalar.copy(out=xi[:, s * HALF : (s + 1) * HALF].rearrange("p (n t) -> p n t", t=PACK), in_=banks[s][:].rearrange("p t n -> p n t"))
-            return xi
+                nc.scalar.copy(out=xi[:, g, s * HALF : (s + 1) * HALF].rearrange("p (n t) -> p n t", t=PACK), in_=banks[s][:].rearrange("p t n -> p n t"))
 
-        def inter_x1(h, gg):
-            xi = packed("x1i")
+        def inter_x1(xi, h, gg):
             nc.vector.tensor_copy(
-                out=xi[:].rearrange("p (u c i t) -> p c u i t", u=PACK, i=2, t=PACK),
+                out=xi[:, gg, :].rearrange("p (u c i t) -> p c u i t", u=PACK, i=2, t=PACK),
                 in_=x1raw[:, h, :, gg * HALF : (gg + 1) * HALF].rearrange("p t (c i u) -> p c u i t", u=PACK, i=2),
             )
-            return xi
 
         def tri(h, g):
             a0 = work.tile([P, PACK, HALF], F32, name="a0", tag="a0")
             a1 = work.tile([P, PACK, HALF], F32, name="a1", bufs=2)
-            r1 = work.tile([P, PACK, HALF], F32, name="r1", bufs=4)
+            r1 = work.tile([P, PACK, HALF], F32, name="r1", tag="r1", bufs=4)
             for t in range(PACK):
                 nc.scalar.activation(out=a0[:, t, :], in_=rows[h, 0][:], func=ACT.Abs, scale=2.0, bias=nb[:, g, 2 * t : 2 * t + 1])
             for t in range(PACK):
@@ -157,13 +171,11 @@ def tile_conleyspatialhaccrossequationmeat_x1_kernel(tc, x1, x2, e1, e2, coord, 
         def clamp(a0):
             nc.vector.tensor_scalar(out=a0[:], in0=a0[:], scalar1=1.0, scalar2=1.0, op0=ALU.min, op1=ALU.subtract)
 
-        def product(a0, r1):
-            ki = packed("kei")
-            nc.vector.tensor_tensor(out=lanes(ki[:]), in0=runs(a0[:]), in1=runs(r1[:]), op=ALU.mult)
-            return ki
+        def product(ki, g, a0, r1):
+            nc.vector.tensor_tensor(out=lanes(ki[:, g, :]), in0=runs(a0[:]), in1=runs(r1[:]), op=ALU.mult)
 
         def mirror_second(a1):
-            r1 = work.tile([P, PACK, HALF], F32, name="r1", bufs=4)
+            r1 = work.tile([P, PACK, HALF], F32, name="r1", tag="r1", bufs=4)
             for t in range(PACK):
                 b = bank(t, [P, PACK, P])
                 for u in range(PACK):
@@ -180,21 +192,16 @@ def tile_conleyspatialhaccrossequationmeat_x1_kernel(tc, x1, x2, e1, e2, coord, 
                 res.append(b)
             return res
 
-        def mirror_product(banks, r1):
-            ki = packed("kei")
+        def mirror_product(ki, banks, r1):
             for u in range(PACK):
-                nc.vector.tensor_tensor(out=lanes(ki[:, u * HALF : (u + 1) * HALF]), in0=runs(banks[u][:]), in1=runs(r1[:, :, u * P : (u + 1) * P]), op=ALU.mult)
-            return ki
+                nc.vector.tensor_tensor(out=lanes(ki[:, 1, u * HALF : (u + 1) * HALF]), in0=runs(banks[u][:]), in1=runs(r1[:, :, u * P : (u + 1) * P]), op=ALU.mult)
 
-        def stage1_narrow(h, qh, first_bank):
-            res = []
-            for s in range(PACK):
-                b = bank(first_bank + s, [P, PACK, P])
-                for u in range(PACK):
-                    for g in range(2):
-                        mx(b[:, u, :], ("k", h, g), u * P, ("x2", g, qh), s * P, P, g == 0, g == 1)
-                res.append(b)
-            return res
+        def stage1_narrow(h, qh, s, k):
+            b = bank(k, [P, PACK, P])
+            for u in range(PACK):
+                for g in range(2):
+                    mx(b[:, u, :], ("k", h, g), u * P, ("x2", g, qh), s * P, P, g == 0, g == 1)
+            return b
 
         def me_narrow(mi, b, h, s):
             nc.vector.tensor_tensor(
@@ -219,100 +226,105 @@ def tile_conleyspatialhaccrossequationmeat_x1_kernel(tc, x1, x2, e1, e2, coord, 
             return mi
 
         t00 = tri(0, 0)
+        p0 = pair("x2i")
         sign_x2(0)
-        p00 = inter_x2(0)
-        clamp(t00[0])
+        inter_x2(p0, 0)
         sign_x2(1)
-        quant(("x2", 0, 0), p00)
-        p10 = inter_x2(1)
+        clamp(t00[0])
+        inter_x2(p0, 1)
         xb0 = x2_banks(0)
         t10 = tri(1, 0)
-        w00 = inter_x1(0, 0)
-        quant(("x2", 1, 0), p10)
-        k00 = product(t00[0], t00[2])
-        w01 = inter_x1(0, 1)
+        w0 = pair("x1i")
+        inter_x1(w0, 0, 0)
+        quant_pair((("x2", 0, 0), ("x2", 1, 0)), p0)
+        k0 = pair("kei")
+        product(k0, 0, t00[0], t00[2])
+        inter_x1(w0, 0, 1)
         clamp(t10[0])
-        quant(("k", 0, 0), k00)
         t11 = tri(1, 1)
         e1s = const.tile([P, 2, PACK], F32, name="e1s")
         nc.vector.tensor_scalar(out=e1s[:], in0=e1col[:], scalar1=INV_ROOT, scalar2=None, op0=ALU.mult)
-        w10 = inter_x1(1, 0)
-        k10 = product(t10[0], t10[2])
-        quant(("x1", 0, 0), w00)
-        w11 = inter_x1(1, 1)
+        w1 = pair("x1i")
+        inter_x1(w1, 1, 0)
+        k1 = pair("kei")
+        product(k1, 0, t10[0], t10[2])
+        quant_pair((("x1", 0, 0), ("x1", 0, 1)), w0)
+        inter_x1(w1, 1, 1)
         clamp(t11[0])
-        quant(("k", 1, 0), k10)
         r01 = mirror_second(t10[1])
         mb = mirror_banks(t10[0])
-        quant(("x1", 0, 1), w01)
-        k11 = product(t11[0], t11[2])
-        quant(("x1", 1, 0), w10)
-        quant(("k", 1, 1), k11)
-        k01 = mirror_product(mb, r01)
-        p01 = x2_out(xb0)
-        p11 = x2_out(x2_banks(1))
-        quant(("x1", 1, 1), w11)
-        quant(("k", 0, 1), k01)
+        quant_pair((("x1", 1, 0), ("x1", 1, 1)), w1)
+        product(k1, 1, t11[0], t11[2])
+        p1 = pair("x2i")
+        x2_out(p1, 0, xb0)
+        x2_out(p1, 1, x2_banks(1))
+        quant_pair((("k", 1, 0), ("k", 1, 1)), k1)
+        mirror_product(k0, mb, r01)
         m10 = packed("mei")
-        nb10 = stage1_narrow(1, 0, 0)
+        nb10 = [stage1_narrow(1, 0, s, s) for s in range(PACK)]
+        quant_pair((("k", 0, 0), ("k", 0, 1)), k0)
+        quant_pair((("x2", 0, 1), ("x2", 1, 1)), p1)
         for s in range(PACK):
             me_narrow(m10, nb10[s], 1, s)
-        quant(("x2", 0, 1), p01)
-        quant(("x2", 1, 1), p11)
         mp00 = me_wide(0, 0, 4)
-        quant(("me", 1, 0), m10)
         m00 = inter_me(mp00)
-        mp01 = me_wide(0, 1, 0)
-        nb11 = stage1_narrow(1, 1, 4)
-        m11 = packed("mei")
-        me_narrow(m11, nb11[0], 1, 0)
+        quant(("me", 1, 0), m10)
         quant(("me", 0, 0), m00)
-        for s in range(1, PACK):
-            me_narrow(m11, nb11[s], 1, s)
-        m01 = inter_me(mp01)
-        quant(("me", 1, 1), m11)
-
-        bank_no = [0]
-
-        def next_bank(shape):
-            bank_no[0] += 1
-            return bank((bank_no[0] - 1) % 8, shape)
+        mp01 = me_wide(0, 1, 4)
+        nb11 = [stage1_narrow(1, 1, s, s) for s in range(3)]
 
         osc = [keep.tile([P, 2, HALF], U8, name="osc%d" % qh, align_bytes=64) for qh in range(2)]
 
-        def product_out(qh, gg, of):
-            for u in range(PACK):
-                b = next_bank([P, HALF])
-                for h in range(2):
-                    mx(b[:], ("x1", h, gg), u * P, ("me", h, qh), 0, HALF, h == 0, h == 1)
-                nc.scalar.activation(out=of[:, u, :], in_=b[:], func=ACT.Copy, scale=INV_ROOT)
+        def product_bank(qh, gg, u, k):
+            b = bank(k, [P, HALF])
+            for h in range(2):
+                mx(b[:], ("x1", h, gg), u * P, ("me", h, qh), 0, HALF, h == 0, h == 1)
+            return b
 
-        def product_out_split(qh, gg, of, part):
-            w = HALF // 2
+        def product_out(qh, gg, banks):
+            of = work.tile([P, PACK, HALF], F32, name="of", tag="a0")
+            view = out_0[gg * HALF : (gg + 1) * HALF, qh * HALF : (qh + 1) * HALF].rearrange("(p t) q -> p t q", t=PACK)
+            for u in range(PACK):
+                nc.scalar.activation(out=of[:, u, :], in_=banks[u][:], func=ACT.Copy, scale=INV_ROOT)
+                nc.sync.dma_start(out=view[:, u, :], in_=of[:, u, :])
+            return of
+
+        def product_out_half(qh, gg, k):
+            of = work.tile([P, PACK, QUARTER], F32, name="ofa", tag="r1", bufs=4)
             for u in range(0, PACK, 2):
-                b = next_bank([P, 2, w])
+                b = bank(k + u // 2, [P, 2, QUARTER])
                 for v in range(2):
                     for h in range(2):
-                        mx(b[:, v, :], ("x1", h, gg), (u + v) * P, ("me", h, qh), part * w, w, h == 0, h == 1)
-                nc.scalar.activation(out=of[:, u : u + 2, part * w : (part + 1) * w], in_=b[:], func=ACT.Copy, scale=INV_ROOT)
+                        mx(b[:, v, :], ("x1", h, gg), (u + v) * P, ("me", h, qh), 0, QUARTER, h == 0, h == 1)
+                nc.scalar.activation(out=of[:, u : u + 2, :], in_=b[:], func=ACT.Copy, scale=INV_ROOT)
+            return of
 
-        def inter_out(of, c0, c1):
-            oi = work.tile([P, HALF * PACK], BF16, name="oi", tag="kei", align_bytes=64)
-            nc.vector.tensor_copy(out=lanes(oi[:, PACK * c0 : PACK * c1]), in_=runs(of[:, :, c0:c1]))
+        def narrow_out(qh, gg, s, k):
+            b = bank(k, [P, PACK, P])
+            for u in range(PACK):
+                for h in range(2):
+                    mx(b[:, u, :], ("x1", h, gg), u * P, ("me", h, qh), s * P, P, h == 0, h == 1)
+            of = work.tile([P, PACK, P], F32, name="ofs", tag="r1", bufs=4)
+            nc.scalar.activation(out=of[:], in_=b[:], func=ACT.Copy, scale=INV_ROOT)
+            return b, of
+
+        def inter_out(of, width):
+            oi = packed("oi")
+            nc.vector.tensor_copy(out=lanes(oi[:, 0 : PACK * width]), in_=runs(of[:]))
             return oi
 
         def store_f32(qh, gg, of, c0, c1):
             q0 = qh * HALF
             nc.sync.dma_start(
-                out=out_0[gg * HALF : (gg + 1) * HALF, q0 + c0 : q0 + c1].rearrange("(p t) q -> p t q", t=PACK), in_=of[:, :, c0:c1]
+                out=out_0[gg * HALF : (gg + 1) * HALF, q0 + c0 : q0 + c1].rearrange("(p t) q -> p t q", t=PACK), in_=of[:]
             )
 
         def finish(qh, gg, oi, c0, c1):
             q0 = qh * HALF
-            oc = work.tile([P, HALF], U32, name="oc", align_bytes=64)
-            nc.vector.quantize_mx(out=oc[:, c0:c1].bitcast(FP8X4), scales=osc[qh][:, gg, c0:c1], in_=oi[:, PACK * c0 : PACK * c1])
+            oc = work.tile([P, HALF], U32, name="oc", bufs=5, align_bytes=64)
+            nc.vector.quantize_mx(out=oc[:, 0 : c1 - c0].bitcast(FP8X4), scales=osc[qh][:, gg, c0:c1], in_=oi[:, 0 : PACK * (c1 - c0)])
             nc.sync.dma_start(
-                out=out_1[gg, :, q0 + c0 : q0 + c1, :].rearrange("p m t -> p (m t)").bitcast(I32), in_=oc[:, c0:c1].bitcast(I32)
+                out=out_1[gg, :, q0 + c0 : q0 + c1, :].rearrange("p m t -> p (m t)").bitcast(I32), in_=oc[:, 0 : c1 - c0].bitcast(I32)
             )
 
         def store_scales(qh):
@@ -324,34 +336,37 @@ def tile_conleyspatialhaccrossequationmeat_x1_kernel(tc, x1, x2, e1, e2, coord, 
                     in_=osc[qh][32 * quad : 32 * quad + 4, :, :].bitcast(I32),
                 )
 
-        def out_tile():
-            return work.tile([P, PACK, HALF], F32, name="of", tag="a0")
-
-        of00 = out_tile()
-        product_out(0, 0, of00)
-        store_f32(0, 0, of00, 0, HALF)
-        of01 = out_tile()
-        product_out(0, 1, of01)
-        store_f32(0, 1, of01, 0, HALF)
-        i00 = inter_out(of00, 0, HALF)
+        banks00 = [product_bank(0, 0, 0, 4)]
+        nb11.append(stage1_narrow(1, 1, 3, 3))
+        m11 = packed("mei")
+        for s in range(PACK):
+            me_narrow(m11, nb11[s], 1, s)
+        m01 = inter_me(mp01)
+        quant(("me", 1, 1), m11)
+        banks00 += [product_bank(0, 0, u, 4 + u) for u in range(1, PACK)]
+        of00 = product_out(0, 0, banks00)
         quant(("me", 0, 1), m01)
+        i00 = inter_out(of00, HALF)
+        of01 = product_out(0, 1, [product_bank(0, 1, u, u) for u in range(PACK)])
+        of10 = product_out(1, 0, [product_bank(1, 0, u, 4 + u) for u in range(PACK)])
         finish(0, 0, i00, 0, HALF)
-        i01 = inter_out(of01, 0, HALF)
-        of10 = out_tile()
-        product_out(1, 0, of10)
-        store_f32(1, 0, of10, 0, HALF)
+        i01 = inter_out(of01, HALF)
         finish(0, 1, i01, 0, HALF)
-        i10 = inter_out(of10, 0, HALF)
-        of11 = out_tile()
-        product_out_split(1, 1, of11, 0)
-        product_out_split(1, 1, of11, 1)
+        ofa = product_out_half(1, 1, 0)
+        store_f32(1, 1, ofa, 0, QUARTER)
         store_scales(0)
-        w = HALF // 2
-        store_f32(1, 1, of11, 0, w)
-        ia = inter_out(of11, 0, w)
+        i10 = inter_out(of10, HALF)
+        b2, of2 = narrow_out(1, 1, 2, 2)
+        b3, of3 = narrow_out(1, 1, 3, 3)
+        store_f32(1, 1, of2, 2 * P, 3 * P)
+        store_f32(1, 1, of3, 3 * P, HALF)
+        ib = packed("oi")
+        nc.scalar.activation(
+            out=ib[:, HALF : 2 * HALF].rearrange("p (n t) -> p n t", t=PACK), in_=b3[:].rearrange("p t n -> p n t"), func=ACT.Copy, scale=INV_ROOT
+        )
+        ia = inter_out(ofa, QUARTER)
         finish(1, 0, i10, 0, HALF)
-        store_f32(1, 1, of11, w, HALF)
-        ib = inter_out(of11, w, HALF)
-        finish(1, 1, ia, 0, w)
-        finish(1, 1, ib, w, HALF)
+        nc.vector.tensor_copy(out=lanes(ib[:, 0:HALF]), in_=runs(of2[:]))
+        finish(1, 1, ia, 0, QUARTER)
+        finish(1, 1, ib, QUARTER, HALF)
         store_scales(1)

from contextlib import ExitStack

import concourse.mybir as mybir
from concourse.masks import make_identity

N = 1024
P = 128
PACK = 4
HALF = 512
QUARTER = 256
FLOPS = 2 * 2 * N * N * N

F32 = mybir.dt.float32
BF16 = mybir.dt.bfloat16
U32 = mybir.dt.uint32
I32 = mybir.dt.int32
U8 = mybir.dt.uint8
FP8X4 = mybir.dt.float8_e4m3fn_x4
ALU = mybir.AluOpType
ACT = mybir.ActivationFunctionType
INV_ROOT = 1.0 / 32.0


def tile_conleyspatialhaccrossequationmeat_x1_kernel(tc, x1, x2, e1, e2, coord, out_0, out_1, out_2):
    nc = tc.nc
    with ExitStack() as ctx:
        const = ctx.enter_context(tc.tile_pool(name="const", bufs=1))
        keep = ctx.enter_context(tc.tile_pool(name="keep", bufs=1))
        work = ctx.enter_context(tc.tile_pool(name="work", bufs=3))
        psum = ctx.enter_context(tc.psum_pool(name="psum", bufs=1))
        ctx.enter_context(tc.manual_schedule())

        ccol = const.tile([P, 2, 2 * PACK], BF16, name="ccol")
        nc.sync.dma_start(out=ccol[:], in_=coord.rearrange("(g p t) c -> p g (t c)", g=2, t=PACK))
        e2col = const.tile([P, 2, PACK], BF16, name="e2col")
        nc.scalar.dma_start(out=e2col[:], in_=e2.rearrange("(g p t) -> p g t", g=2, t=PACK))
        x2lo = [keep.tile([P, PACK, HALF], BF16, name="x2lo%d" % g) for g in range(2)]
        x2hi = [keep.tile([P, PACK, HALF], BF16, name="x2hi%d" % g) for g in range(2)]
        x1raw = keep.tile([P, 2, PACK, N], BF16, name="x1raw")
        x2view = x2.rearrange("(g p t) w -> g p t w", g=2, t=PACK)
        x1view = x1.rearrange("(g p t) w -> g p t w", g=2, t=PACK)
        for g in range(2):
            nc.sync.dma_start(out=x2lo[g][:], in_=x2view[g, :, :, 0:HALF])
        for g in range(2):
            for t2 in range(2):
                nc.sync.dma_start(out=x1raw[:, g, 2 * t2 : 2 * t2 + 2, :], in_=x1view[g, :, 2 * t2 : 2 * t2 + 2, :])
        for g in range(2):
            nc.sync.dma_start(out=x2hi[g][:], in_=x2view[g, :, :, HALF:N])
        e1col = const.tile([P, 2, PACK], BF16, name="e1col")
        nc.sync.dma_start(out=e1col[:], in_=e1.rearrange("(g p t) -> p g t", g=2, t=PACK))

        ident = const.tile([P, P], BF16, name="ident")
        make_identity(nc, ident[:])
        ident_f = const.tile([P, P], F32, name="ident_f")
        make_identity(nc, ident_f[:])
        ones = const.tile([P, P], BF16, name="ones")
        nc.vector.memset(ones[:], 1.0)

        def bank(k, shape):
            return psum.tile(shape, F32, name="bank", tag="b%d" % k)

        rows = {}

        def make_row(h, c):
            diag = work.tile([P, PACK, P], BF16, name="diag", bufs=4)
            for u in range(PACK):
                k = 2 * u + c
                nc.vector.tensor_scalar(out=diag[:, u, :], in0=ident[:], scalar1=ccol[:, h, k : k + 1], scalar2=None, op0=ALU.mult)
            rows[h, c] = bank(2 * h + c, [P, HALF])
            nc.tensor.matmul(rows[h, c][:], ones[:], diag[:].rearrange("p u m -> p (u m)"), start=True, stop=True)

        nb = const.tile([P, 2, 2 * PACK], F32, name="nb")
        nc.vector.tensor_scalar(out=nb[:], in0=ccol[:], scalar1=-2.0, scalar2=None, op0=ALU.mult)
        make_row(0, 0)
        make_row(0, 1)
        ae2 = const.tile([P, 2, PACK], F32, name="ae2")
        nc.vector.scalar_tensor_tensor(out=ae2[:], in0=e2col[:], scalar=-1.0, in1=e2col[:], op0=ALU.mult, op1=ALU.max)
        sg = const.tile([P, 2, PACK], F32, name="sg")
        nc.vector.tensor_scalar(out=sg[:], in0=e2col[:], scalar1=0.0, scalar2=-2.0, op0=ALU.is_ge, op1=ALU.mult)
        nae2 = const.tile([P, 2, PACK], F32, name="nae2")
        nc.vector.tensor_scalar(out=nae2[:], in0=ae2[:], scalar1=-1.0, scalar2=None, op0=ALU.mult)
        nsg = const.tile([P, 2, PACK], F32, name="nsg")
        nc.vector.tensor_scalar(out=nsg[:], in0=sg[:], scalar1=1.0, scalar2=None, op0=ALU.add)
        make_row(1, 0)
        make_row(1, 1)
        sdiag = const.tile([P, 2, PACK, P], BF16, name="sdiag")
        for g in range(2):
            for t in range(PACK):
                nc.gpsimd.tensor_scalar(out=sdiag[:, g, t, :], in0=ident[:], scalar1=nsg[:, g, t : t + 1], scalar2=1.0, op0=ALU.mult, op1=ALU.mult)

        codes, scales = {}, {}

        def quant(key, src):
            codes[key] = keep.tile([P, HALF], U32, name="c_%s%d%d" % key, align_bytes=64)
            scales[key] = keep.tile([P, HALF], U8, name="s_%s%d%d" % key, align_bytes=64)
            nc.vector.quantize_mx(out=codes[key][:].bitcast(FP8X4), scales=scales[key][:], in_=src[:])

        def quant_pair(keys, src):
            ct = keep.tile([P, 2, HALF], U32, name="c_%s%d%d" % keys[0], align_bytes=64)
            st = keep.tile([P, 2, HALF], U8, name="s_%s%d%d" % keys[0], align_bytes=64)
            nc.vector.quantize_mx(
                out=ct[:].rearrange("p k n -> p (k n)").bitcast(FP8X4),
                scales=st[:].rearrange("p k n -> p (k n)"),
                in_=src[:].rearrange("p k n -> p (k n)"),
            )
            for k in range(2):
                codes[keys[k]] = ct[:, k, :]
                scales[keys[k]] = st[:, k, :]

        def mx(out, lkey, lcol, rkey, rcol, rn, first, last):
            nc.tensor.matmul_mx(
                out=out,
                lhsT=codes[lkey][:, lcol : lcol + P].bitcast(FP8X4),
                lhsT_scale=scales[lkey][:, lcol : lcol + P],
                rhs=codes[rkey][:, rcol : rcol + rn].bitcast(FP8X4),
                rhs_scale=scales[rkey][:, rcol : rcol + rn],
                start=first,
                stop=last,
            )

        def lanes(ap):
            return ap.rearrange("p (c i t) -> p c t i", t=PACK, i=4)

        def runs(ap):
            return ap.rearrange("p t (c i) -> p c t i", i=4)

        def packed(name):
            return work.tile([P, HALF * PACK], BF16, name=name, align_bytes=64)

        def pair(name):
            return work.tile([P, 2, HALF * PACK], BF16, name=name, tag="pair", bufs=5, align_bytes=64)

        def sign_x2(g):
            for t in range(PACK):
                nc.vector.tensor_scalar(out=x2lo[g][:, t, :], in0=x2lo[g][:, t, :], scalar1=nsg[:, g, t : t + 1], scalar2=None, op0=ALU.mult)

        def inter_x2(xi, g):
            nc.vector.tensor_copy(out=lanes(xi[:, g, :]), in_=runs(x2lo[g][:]))

        def x2_banks(g):
            res = []
            for s in range(PACK):
                b = bank(4 + s, [P, PACK, P])
                for t in range(PACK):
                    nc.tensor.matmul(b[:, t, :], sdiag[:, g, t, :], x2hi[g][:, t, s * P : (s + 1) * P], start=True, stop=True)
                res.append(b)
            return res

        def x2_out(xi, g, banks):
            for s in range(PACK):
                nc.scalar.copy(out=xi[:, g, s * HALF : (s + 1) * HALF].rearrange("p (n t) -> p n t", t=PACK), in_=banks[s][:].rearrange("p t n -> p n t"))

        def inter_x1(xi, h, gg):
            nc.vector.tensor_copy(
                out=xi[:, gg, :].rearrange("p (u c i t) -> p c u i t", u=PACK, i=2, t=PACK),
                in_=x1raw[:, h, :, gg * HALF : (gg + 1) * HALF].rearrange("p t (c i u) -> p c u i t", u=PACK, i=2),
            )

        def tri(h, g):
            a0 = work.tile([P, PACK, HALF], F32, name="a0", tag="a0")
            a1 = work.tile([P, PACK, HALF], F32, name="a1", bufs=2)
            r1 = work.tile([P, PACK, HALF], F32, name="r1", tag="r1", bufs=4)
            for t in range(PACK):
                nc.scalar.activation(out=a0[:, t, :], in_=rows[h, 0][:], func=ACT.Abs, scale=2.0, bias=nb[:, g, 2 * t : 2 * t + 1])
            for t in range(PACK):
                nc.scalar.activation(out=a1[:, t, :], in_=rows[h, 1][:], func=ACT.Abs, scale=2.0, bias=nb[:, g, 2 * t + 1 : 2 * t + 2])
            for t in range(PACK):
                nc.scalar.activation(out=r1[:, t, :], in_=a1[:, t, :], func=ACT.Relu, scale=nae2[:, g, t : t + 1], bias=ae2[:, g, t : t + 1])
            return a0, a1, r1

        def clamp(a0):
            nc.vector.tensor_scalar(out=a0[:], in0=a0[:], scalar1=1.0, scalar2=1.0, op0=ALU.min, op1=ALU.subtract)

        def product(ki, g, a0, r1):
            nc.vector.tensor_tensor(out=lanes(ki[:, g, :]), in0=runs(a0[:]), in1=runs(r1[:]), op=ALU.mult)

        def mirror_second(a1):
            r1 = work.tile([P, PACK, HALF], F32, name="r1", tag="r1", bufs=4)
            for t in range(PACK):
                b = bank(t, [P, PACK, P])
                for u in range(PACK):
                    nc.tensor.transpose(b[:, u, :], a1[:, u, t * P : (t + 1) * P], ident_f[:])
                nc.scalar.activation(out=r1[:, t, :], in_=b[:].rearrange("p u m -> p (u m)"), func=ACT.Relu, scale=nae2[:, 1, t : t + 1], bias=ae2[:, 1, t : t + 1])
            return r1

        def mirror_banks(a0):
            res = []
            for u in range(PACK):
                b = bank(u, [P, PACK, P])
                for t in range(PACK):
                    nc.tensor.transpose(b[:, t, :], a0[:, u, t * P : (t + 1) * P], ident_f[:])
                res.append(b)
            return res

        def mirror_product(ki, banks, r1):
            for u in range(PACK):
                nc.vector.tensor_tensor(out=lanes(ki[:, 1, u * HALF : (u + 1) * HALF]), in0=runs(banks[u][:]), in1=runs(r1[:, :, u * P : (u + 1) * P]), op=ALU.mult)

        def stage1_narrow(h, qh, s, k):
            b = bank(k, [P, PACK, P])
            for u in range(PACK):
                for g in range(2):
                    mx(b[:, u, :], ("k", h, g), u * P, ("x2", g, qh), s * P, P, g == 0, g == 1)
            return b

        def me_narrow(mi, b, h, s):
            nc.vector.tensor_tensor(
                out=mi[:, s * HALF : (s + 1) * HALF].rearrange("p (n t) -> p n t", t=PACK),
                in0=b[:].rearrange("p t n -> p n t"),
                in1=e1s[:, h : h + 1, :].to_broadcast([P, P, PACK]),
                op=ALU.mult,
            )

        def me_wide(h, qh, first_bank):
            mp = work.tile([P, PACK, HALF], BF16, name="mp", bufs=2)
            for u in range(PACK):
                b = bank(first_bank + u, [P, HALF])
                for g in range(2):
                    mx(b[:], ("k", h, g), u * P, ("x2", g, qh), 0, HALF, g == 0, g == 1)
                nc.scalar.activation(out=mp[:, u, :], in_=b[:], func=ACT.Copy, scale=e1s[:, h, u : u + 1])
            return mp

        def inter_me(mp):
            mi = packed("mei")
            nc.vector.tensor_copy(out=lanes(mi[:]), in_=runs(mp[:]))
            return mi

        t00 = tri(0, 0)
        p0 = pair("x2i")
        sign_x2(0)
        inter_x2(p0, 0)
        sign_x2(1)
        clamp(t00[0])
        inter_x2(p0, 1)
        xb0 = x2_banks(0)
        t10 = tri(1, 0)
        w0 = pair("x1i")
        inter_x1(w0, 0, 0)
        quant_pair((("x2", 0, 0), ("x2", 1, 0)), p0)
        k0 = pair("kei")
        product(k0, 0, t00[0], t00[2])
        inter_x1(w0, 0, 1)
        clamp(t10[0])
        t11 = tri(1, 1)
        e1s = const.tile([P, 2, PACK], F32, name="e1s")
        nc.vector.tensor_scalar(out=e1s[:], in0=e1col[:], scalar1=INV_ROOT, scalar2=None, op0=ALU.mult)
        w1 = pair("x1i")
        inter_x1(w1, 1, 0)
        k1 = pair("kei")
        product(k1, 0, t10[0], t10[2])
        quant_pair((("x1", 0, 0), ("x1", 0, 1)), w0)
        inter_x1(w1, 1, 1)
        clamp(t11[0])
        r01 = mirror_second(t10[1])
        mb = mirror_banks(t10[0])
        quant_pair((("x1", 1, 0), ("x1", 1, 1)), w1)
        product(k1, 1, t11[0], t11[2])
        p1 = pair("x2i")
        x2_out(p1, 0, xb0)
        x2_out(p1, 1, x2_banks(1))
        quant_pair((("k", 1, 0), ("k", 1, 1)), k1)
        mirror_product(k0, mb, r01)
        m10 = packed("mei")
        nb10 = [stage1_narrow(1, 0, s, s) for s in range(PACK)]
        quant_pair((("k", 0, 0), ("k", 0, 1)), k0)
        quant_pair((("x2", 0, 1), ("x2", 1, 1)), p1)
        for s in range(PACK):
            me_narrow(m10, nb10[s], 1, s)
        mp00 = me_wide(0, 0, 4)
        m00 = inter_me(mp00)
        quant(("me", 1, 0), m10)
        quant(("me", 0, 0), m00)
        mp01 = me_wide(0, 1, 4)
        nb11 = [stage1_narrow(1, 1, s, s) for s in range(3)]

        osc = [keep.tile([P, 2, HALF], U8, name="osc%d" % qh, align_bytes=64) for qh in range(2)]

        def product_bank(qh, gg, u, k):
            b = bank(k, [P, HALF])
            for h in range(2):
                mx(b[:], ("x1", h, gg), u * P, ("me", h, qh), 0, HALF, h == 0, h == 1)
            return b

        def product_out(qh, gg, banks):
            of = work.tile([P, PACK, HALF], F32, name="of", tag="a0")
            view = out_0[gg * HALF : (gg + 1) * HALF, qh * HALF : (qh + 1) * HALF].rearrange("(p t) q -> p t q", t=PACK)
            for u in range(PACK):
                nc.scalar.activation(out=of[:, u, :], in_=banks[u][:], func=ACT.Copy, scale=INV_ROOT)
                nc.sync.dma_start(out=view[:, u, :], in_=of[:, u, :])
            return of

        def product_out_half(qh, gg, k):
            of = work.tile([P, PACK, QUARTER], F32, name="ofa", tag="r1", bufs=4)
            for u in range(0, PACK, 2):
                b = bank(k + u // 2, [P, 2, QUARTER])
                for v in range(2):
                    for h in range(2):
                        mx(b[:, v, :], ("x1", h, gg), (u + v) * P, ("me", h, qh), 0, QUARTER, h == 0, h == 1)
                nc.scalar.activation(out=of[:, u : u + 2, :], in_=b[:], func=ACT.Copy, scale=INV_ROOT)
            return of

        def narrow_out(qh, gg, s, k):
            b = bank(k, [P, PACK, P])
            for u in range(PACK):
                for h in range(2):
                    mx(b[:, u, :], ("x1", h, gg), u * P, ("me", h, qh), s * P, P, h == 0, h == 1)
            of = work.tile([P, PACK, P], F32, name="ofs", tag="r1", bufs=4)
            nc.scalar.activation(out=of[:], in_=b[:], func=ACT.Copy, scale=INV_ROOT)
            return b, of

        def inter_out(of, width):
            oi = packed("oi")
            nc.vector.tensor_copy(out=lanes(oi[:, 0 : PACK * width]), in_=runs(of[:]))
            return oi

        def store_f32(qh, gg, of, c0, c1):
            q0 = qh * HALF
            nc.sync.dma_start(
                out=out_0[gg * HALF : (gg + 1) * HALF, q0 + c0 : q0 + c1].rearrange("(p t) q -> p t q", t=PACK), in_=of[:]
            )

        def finish(qh, gg, oi, c0, c1):
            q0 = qh * HALF
            oc = work.tile([P, HALF], U32, name="oc", bufs=5, align_bytes=64)
            nc.vector.quantize_mx(out=oc[:, 0 : c1 - c0].bitcast(FP8X4), scales=osc[qh][:, gg, c0:c1], in_=oi[:, 0 : PACK * (c1 - c0)])
            nc.sync.dma_start(
                out=out_1[gg, :, q0 + c0 : q0 + c1, :].rearrange("p m t -> p (m t)").bitcast(I32), in_=oc[:, 0 : c1 - c0].bitcast(I32)
            )

        def store_scales(qh):
            q0 = qh * HALF
            for quad in range(4):
                eng = nc.sync if quad % 2 == 0 else nc.scalar
                eng.dma_start(
                    out=out_2[:, 4 * quad : 4 * quad + 4, q0 : q0 + HALF].rearrange("g r m -> r g m").bitcast(I32),
                    in_=osc[qh][32 * quad : 32 * quad + 4, :, :].bitcast(I32),
                )

        banks00 = [product_bank(0, 0, 0, 4)]
        nb11.append(stage1_narrow(1, 1, 3, 3))
        m11 = packed("mei")
        for s in range(PACK):
            me_narrow(m11, nb11[s], 1, s)
        m01 = inter_me(mp01)
        quant(("me", 1, 1), m11)
        banks00 += [product_bank(0, 0, u, 4 + u) for u in range(1, PACK)]
        of00 = product_out(0, 0, banks00)
        quant(("me", 0, 1), m01)
        i00 = inter_out(of00, HALF)
        of01 = product_out(0, 1, [product_bank(0, 1, u, u) for u in range(PACK)])
        of10 = product_out(1, 0, [product_bank(1, 0, u, 4 + u) for u in range(PACK)])
        finish(0, 0, i00, 0, HALF)
        i01 = inter_out(of01, HALF)
        finish(0, 1, i01, 0, HALF)
        ofa = product_out_half(1, 1, 0)
        store_f32(1, 1, ofa, 0, QUARTER)
        store_scales(0)
        i10 = inter_out(of10, HALF)
        b2, of2 = narrow_out(1, 1, 2, 2)
        b3, of3 = narrow_out(1, 1, 3, 3)
        store_f32(1, 1, of2, 2 * P, 3 * P)
        store_f32(1, 1, of3, 3 * P, HALF)
        ib = packed("oi")
        nc.scalar.activation(
            out=ib[:, HALF : 2 * HALF].rearrange("p (n t) -> p n t", t=PACK), in_=b3[:].rearrange("p t n -> p n t"), func=ACT.Copy, scale=INV_ROOT
        )
        ia = inter_out(ofa, QUARTER)
        finish(1, 0, i10, 0, HALF)
        nc.vector.tensor_copy(out=lanes(ib[:, 0:HALF]), in_=runs(of2[:]))
        finish(1, 1, ia, 0, QUARTER)
        finish(1, 1, ib, QUARTER, HALF)
        store_scales(1)
